import numpy as np
import ml_dtypes


def mxq(x, axis, fmt="e4m3"):
    dtype, down = {"e4m3": (ml_dtypes.float8_e4m3fn, 7), "e5m2": (ml_dtypes.float8_e5m2, 14)}[fmt]
    v = np.moveaxis(np.asarray(x, np.float32).astype(ml_dtypes.bfloat16).astype(np.float64), axis, -1)
    blocks = v.reshape(v.shape[:-1] + (-1, 32))
    amax = np.abs(blocks).max(-1, keepdims=True)
    byte = np.maximum(np.where(amax > 0, np.frexp(amax)[1] - 1 + 127, 0) - down, 1)
    scale = np.exp2(byte - 127.0)
    codes = (blocks / scale).astype(np.float32).astype(dtype).astype(np.float64)
    return np.moveaxis((codes * scale).reshape(v.shape), -1, axis)


WIDE = False


def mx_kscale(k):
    if not WIDE:
        return np.ones(k)
    levels = np.array([10, -10, 5, -5, 0])
    if k % 512:
        return np.exp2(np.random.permutation(np.resize(levels, k // 32))).repeat(32)
    a = np.empty((k // 512, 16))
    for p in range(k // 512):
        a[p, :8] = np.random.permutation(np.resize(levels, 8))
        for g in range(8):
            far = levels[np.abs(levels - a[p, g]) >= 10]
            a[p, g + 8] = far[np.random.randint(len(far))]
    return np.exp2(a.ravel()).repeat(32)


def f64(x):
    return np.asarray(x).astype(np.float64)


def striped(idx):
    return np.tile(np.asarray(idx).reshape(-1, 16).T, (8, 1)).astype(np.uint16)


def unstriped(offs):
    return offs[:16].T.reshape(-1).astype(np.int64)


E2M1 = np.array([0.0, 0.5, 1.0, 1.5, 2.0, 3.0, 4.0, 6.0, -0.0, -0.5, -1.0, -1.5, -2.0, -3.0, -4.0, -6.0])


def pack_weight(w, fmt):
    k, n = w.shape
    w = f64(np.asarray(w, np.float32).astype(ml_dtypes.bfloat16)).reshape(k // 32, 32, n)
    amax = np.abs(w).max(1)
    if fmt == "e4m3":
        byte = np.frexp(amax)[1] - 1 + 127 - 7
    else:
        mant, ex = np.frexp(amax / 6.0)
        byte = np.where(mant > 0.5, ex, ex - 1) + 127
    byte = np.clip(np.where(amax > 0, byte, 1), 1, 254)
    scaled = (w * np.exp2(127.0 - byte)[:, None, :]).reshape(k, n).astype(np.float32)
    by_word = np.ascontiguousarray(scaled.reshape(k // 512, 128, 4, n).transpose(0, 1, 3, 2))
    if fmt == "e4m3":
        words = by_word.astype(ml_dtypes.float8_e4m3fn).view(np.uint8)
    else:
        c = by_word.astype(ml_dtypes.float4_e2m1fn).view(np.uint8) & 0xF
        words = (c[..., 0::2] | (c[..., 1::2] << 4)).reshape(k // 512, 128, 2 * n)
    return np.ascontiguousarray(words), np.ascontiguousarray(byte.astype(np.uint8).reshape(k // 512, 16, n))


def unpack_weight(words, scales, fmt):
    g, _, n = scales.shape
    words = np.ascontiguousarray(words).reshape(g, 128, n, -1)
    if fmt == "e4m3":
        vals = words.view(ml_dtypes.float8_e4m3fn).astype(np.float64)
    else:
        nib = np.empty((g, 128, n, 4), np.uint8)
        nib[..., 0::2] = words & 0xF
        nib[..., 1::2] = words >> 4
        vals = E2M1[nib]
    vals = vals * np.repeat(np.exp2(scales.astype(np.float64) - 127.0), 8, axis=1)[..., None]
    return vals.transpose(0, 1, 3, 2).reshape(g * 512, n)


D, T, I, Q, E, M = 512, 1024, 512, 512, 512, 1024


def setup_inputs():
    n = np.random.standard_normal
    idx = np.random.permutation(T)[:I]
    idx2 = np.random.permutation(T)[:I]
    idx3 = np.random.permutation(T)[:I]
    idx4 = np.random.permutation(M)[:I]
    fd = mx_kscale(D)
    fq = mx_kscale(Q)
    keysp = pack_weight(n((D, T)) / fd[:, None], "e2m1")
    return {
        "query": (n((D, Q)) * 0.9 / np.sqrt(D) * fd[:, None]).astype(np.float32),
        "keys_words": keysp[0],
        "keys_scales": keysp[1],
        "lam": (np.random.uniform(0.3, 0.9, (Q, 1))).astype(np.float32),
        "qs": (np.random.uniform(0.5, 2.0, (Q, 1)) * fq[:, None]).astype(np.float32),
        "msgs": (n((Q, E)) * 1 / np.sqrt(Q) / fq[:, None]).astype(np.float32),
        "old": (n((E, M)) * 1.0).astype(np.float32),
        "fade": (np.random.uniform(0.3, 0.9, (1, M))).astype(np.float32),
        "offs": striped(idx),
        "offs2": striped(idx2),
        "offs3": striped(idx3),
        "offs4": striped(idx4),
    }


def reference(query, keys_words, keys_scales, lam, qs, msgs, old, fade, offs, offs2, offs3, offs4):
    idx = unstriped(offs)
    idx2 = unstriped(offs2)
    idx3 = unstriped(offs3)
    idx4 = unstriped(offs4)
    keysu = unpack_weight(keys_words, keys_scales, "e2m1")
    queryq = mxq(f64(query), 0, "e4m3")
    a = queryq.T @ keysu
    w = a[:, idx] + np.maximum(a[:, idx2], a[:, idx3]) * f64(lam)
    wq = w * f64(qs)
    msgsq = mxq(f64(msgs), 0, "e4m3")
    wqq = mxq(wq, 0, "e4m3")
    dl = msgsq.T @ wqq
    df = np.zeros((E, M))
    df[:, idx4] = dl
    y = f64(old) * f64(fade) + df
    return y

@@ -1,0 +1,240 @@
+from contextlib import ExitStack
+
+import concourse.mybir as mybir
+from concourse.masks import make_identity
+
+D, T, I, Q, E, M = 512, 1024, 512, 512, 512, 1024
+FLOPS = 2 * D * Q * T + 2 * Q * E * I
+
+F32 = mybir.dt.float32
+BF16 = mybir.dt.bfloat16
+I32 = mybir.dt.int32
+U32 = mybir.dt.uint32
+U16 = mybir.dt.uint16
+U8 = mybir.dt.uint8
+FP8X4 = mybir.dt.float8_e4m3fn_x4
+FP4X4 = mybir.dt.float4_e2m1fn_x4
+MULT = mybir.AluOpType.mult
+ADD = mybir.AluOpType.add
+MAX = mybir.AluOpType.max
+COPY = mybir.ActivationFunctionType.Copy
+
+P = 128
+PACK = 4
+BANK = 512
+HALF = I // 2
+LIST_COLS = I // 16
+
+
+def tile_attend_lookahead_delivered_lean_kernel(
+    tc, query, keys_words, keys_scales, lam, qs, msgs, old, fade, offs, offs2, offs3, offs4, out
+):
+    nc = tc.nc
+    with ExitStack() as ctx:
+        keep = ctx.enter_context(tc.tile_pool(name="keep", bufs=1))
+        psum_fade = ctx.enter_context(tc.psum_pool(name="psum_fade", bufs=1))
+        psum = ctx.enter_context(tc.psum_pool(name="psum", bufs=6))
+
+        def tiles(name, count, shape, dtype):
+            return [keep.tile(shape, dtype, name="%s%d" % (name, n), align_bytes=64) for n in range(count)]
+
+        key_scales = keep.tile([P, T], U8, align_bytes=64)
+        nc.vector.memset(key_scales[:].bitcast(I32), 0)
+        for quad in range(4):
+            nc.scalar.dma_start(
+                out=key_scales[32 * quad : 32 * quad + 4, :].bitcast(I32),
+                in_=keys_scales[0, 4 * quad : 4 * quad + 4, :].bitcast(I32),
+            )
+        query_raw = keep.tile([P, PACK, Q], F32)
+        nc.sync.dma_start(out=query_raw[:], in_=query.rearrange("(p j) q -> p j q", j=PACK))
+        key_words = keep.tile([P, 2 * T], U8, align_bytes=64)
+        nc.sync.dma_start(out=key_words[:].bitcast(I32), in_=keys_words[0].bitcast(I32))
+        second = keep.tile([P, LIST_COLS], U16)
+        nc.sync.dma_start(second[:], offs2)
+        third = keep.tile([P, LIST_COLS], U16)
+        nc.sync.dma_start(third[:], offs3)
+        first = keep.tile([P, LIST_COLS], U16)
+        nc.sync.dma_start(first[:], offs)
+        lam_sb = keep.tile([P, PACK], F32)
+        nc.sync.dma_start(out=lam_sb[:], in_=lam.rearrange("(p r) o -> p (r o)", r=PACK))
+        qs_sb = keep.tile([P, PACK], F32)
+        nc.sync.dma_start(out=qs_sb[:], in_=qs.rearrange("(p r) o -> p (r o)", r=PACK))
+        fade_sb = keep.tile([P, 2, PACK], F32)
+        nc.sync.dma_start(out=fade_sb[:], in_=fade.rearrange("o (h p k) -> p (o h) k", h=2, k=PACK))
+        msgs_raw = keep.tile([P, PACK, E], F32)
+        nc.sync.dma_start(out=msgs_raw[:], in_=msgs.rearrange("(p r) e -> p r e", r=PACK))
+        places = keep.tile([P, LIST_COLS], U16)
+        nc.sync.dma_start(places[:], offs4)
+        kept = tiles("kept", 4, [P, M], F32)
+        for et in range(4):
+            nc.sync.dma_start(out=kept[et][:], in_=old[P * et : P * (et + 1), :])
+
+        ident = keep.tile([P, P], F32)
+        make_identity(nc, ident[:])
+        delivered = tiles("delivered", 4, [P, M], F32)
+        for et in range(4):
+            nc.vector.memset(delivered[et][:], 0.0)
+
+        query_bf = tiles("query_bf", PACK, [P, P, PACK], BF16)
+        query_codes = tiles("query_codes", PACK, [P, P], U32)
+        query_scales = tiles("query_scales", PACK, [P, P], U8)
+        scores = tiles("scores", PACK, [P, T], F32)
+        own = tiles("own", PACK, [P, I], F32)
+        next_a = tiles("next_a", PACK, [P, I], F32)
+        next_b = tiles("next_b", PACK, [P, I], F32)
+        larger = tiles("larger", PACK, [P, I], F32)
+        weight = tiles("weight", PACK, [P, I], F32)
+        planes = tiles("planes", 2, [P, PACK, HALF], BF16)
+        wq_bf = tiles("wq_bf", 2, [P, HALF, PACK], BF16)
+        wq_codes = tiles("wq_codes", 2, [P, HALF], U32)
+        wq_scales = tiles("wq_scales", 2, [P, HALF], U8)
+        msgs_bf = keep.tile([P, E, PACK], BF16, align_bytes=64)
+        msgs_codes = keep.tile([P, E], U32, align_bytes=64)
+        msgs_scales = keep.tile([P, E], U8, align_bytes=64)
+        sums = tiles("sums", 4, [P, 2, HALF], F32)
+        fade_rows = [psum_fade.tile([P, PACK, P], F32, name="fade_rows%d" % h) for h in range(2)]
+
+        def lay_query(r, engine):
+            src = query_raw[:].rearrange("p j (s r) -> p r s j", r=PACK)[:, r]
+            if engine == "vector":
+                nc.vector.tensor_copy(out=query_bf[r][:], in_=src)
+            else:
+                nc.scalar.copy(out=query_bf[r][:], in_=src)
+
+        def quantize(codes, scales, values):
+            nc.vector.quantize_mx(
+                out=codes[:].bitcast(FP8X4), scales=scales[:], in_=values[:].rearrange("p n j -> p (n j)")
+            )
+
+        def score(r, engines):
+            for h in range(2):
+                bank = psum.tile([P, BANK], F32, name="bank")
+                nc.tensor.matmul_mx(
+                    out=bank[:],
+                    lhsT=query_codes[r][:].bitcast(FP8X4),
+                    lhsT_scale=query_scales[r][:],
+                    rhs=key_words[:, 2 * BANK * h : 2 * BANK * (h + 1)].bitcast(FP4X4),
+                    rhs_scale=key_scales[:, BANK * h : BANK * (h + 1)],
+                    start=True,
+                    stop=True,
+                )
+                dst = scores[r][:, BANK * h : BANK * (h + 1)]
+                if engines[h] == "vector":
+                    nc.vector.tensor_copy(out=dst, in_=bank[:])
+                else:
+                    nc.scalar.copy(out=dst, in_=bank[:])
+
+        def look_up(r, dst, offsets, engine, lo, hi):
+            window = scores[r][:].indirect(offsets[:, lo // 16 : hi // 16])
+            if engine == "vector":
+                nc.vector.tensor_copy(dst[r][:, lo:hi], window)
+            else:
+                nc.scalar.activation(dst[r][:, lo:hi], window, COPY)
+
+        def look_up_all(r, lo, hi, own_engine):
+            look_up(r, next_a, second, "scalar", lo, hi)
+            look_up(r, next_b, third, "scalar", lo, hi)
+            look_up(r, own, first, own_engine, lo, hi)
+
+        def combine(r, lo, hi):
+            nc.vector.tensor_tensor(larger[r][:, lo:hi], next_a[r][:, lo:hi], next_b[r][:, lo:hi], MAX)
+            nc.vector.scalar_tensor_tensor(
+                weight[r][:, lo:hi], larger[r][:, lo:hi], lam_sb[:, r : r + 1], own[r][:, lo:hi], MULT, ADD
+            )
+            for h in range(lo // HALF, hi // HALF):
+                nc.vector.tensor_scalar(
+                    planes[h][:, r, :], weight[r][:, HALF * h : HALF * (h + 1)], qs_sb[:, r : r + 1], None, MULT
+                )
+
+        def quantize_weights(h):
+            nc.vector.tensor_copy(out=wq_bf[h][:], in_=planes[h][:].rearrange("p r i -> p i r"))
+            quantize(wq_codes[h], wq_scales[h], wq_bf[h])
+
+        def carry(h, pair, engine):
+            bank = psum.tile([P, 2, HALF], F32, name="bank")
+            for n in range(2):
+                cols = slice(P * (2 * pair + n), P * (2 * pair + n + 1))
+                nc.tensor.matmul_mx(
+                    out=bank[:, n, :],
+                    lhsT=msgs_codes[:, cols].bitcast(FP8X4),
+                    lhsT_scale=msgs_scales[:, cols],
+                    rhs=wq_codes[h][:].bitcast(FP8X4),
+                    rhs_scale=wq_scales[h][:],
+                    start=True,
+                    stop=True,
+                )
+            dst = sums[2 * h + pair][:]
+            if engine == "vector":
+                nc.vector.tensor_copy(out=dst, in_=bank[:])
+            else:
+                nc.scalar.copy(out=dst, in_=bank[:])
+
+        def deliver(et, h, engine):
+            window = delivered[et][:].indirect(places[:, HALF * h // 16 : HALF * (h + 1) // 16])
+            src = sums[2 * h + et // 2][:, et % 2, :]
+            if engine == "vector":
+                nc.vector.tensor_copy(window, src)
+            else:
+                nc.scalar.activation(window, src, COPY)
+
+        def fade_old(et):
+            for h in range(2):
+                part = kept[et][:, BANK * h : BANK * (h + 1)].rearrange("p (n k) -> p n k", k=PACK)
+                nc.vector.tensor_tensor(part, part, fade_rows[h][:].rearrange("p k n -> p n k"), MULT)
+
+        def finish(et, pieces):
+            width = M // pieces
+            for n in range(pieces):
+                cols = slice(width * n, width * (n + 1))
+                nc.vector.tensor_tensor(kept[et][:, cols], kept[et][:, cols], delivered[et][:, cols], ADD)
+                nc.sync.dma_start(out=out[P * et : P * (et + 1), cols], in_=kept[et][:, cols])
+
+        lay_query(0, "vector")
+        lay_query(1, "scalar")
+        quantize(query_codes[0], query_scales[0], query_bf[0])
+        lay_query(2, "vector")
+        quantize(query_codes[1], query_scales[1], query_bf[1])
+        score(0, ("vector", "scalar"))
+        look_up_all(0, 0, I, "vector")
+        lay_query(3, "vector")
+        quantize(query_codes[2], query_scales[2], query_bf[2])
+        quantize(query_codes[3], query_scales[3], query_bf[3])
+        score(1, ("scalar", "scalar"))
+        for h in range(2):
+            for k in range(PACK):
+                nc.tensor.transpose(fade_rows[h][:, k, :], fade_sb[:, h, k : k + 1].to_broadcast([P, P]), ident[:])
+        combine(0, 0, I)
+        look_up_all(1, 0, I, "vector")
+        score(2, ("scalar", "scalar"))
+        nc.vector.tensor_copy(out=msgs_bf[:], in_=msgs_raw[:].rearrange("p r e -> p e r"))
+        combine(1, 0, I)
+        quantize(msgs_codes, msgs_scales, msgs_bf)
+        look_up_all(2, 0, I, "vector")
+        score(3, ("scalar", "scalar"))
+        fade_old(0)
+        combine(2, 0, I)
+        look_up_all(3, 0, HALF, "vector")
+        fade_old(1)
+        combine(3, 0, HALF)
+        look_up_all(3, HALF, I, "scalar")
+        quantize_weights(0)
+        carry(0, 0, "scalar")
+        deliver(0, 0, "scalar")
+        deliver(1, 0, "scalar")
+        combine(3, HALF, I)
+        quantize_weights(1)
+        carry(1, 0, "vector")
+        deliver(0, 1, "vector")
+        deliver(1, 1, "scalar")
+        finish(0, 1)
+        carry(0, 1, "scalar")
+        deliver(2, 0, "scalar")
+        finish(1, 1)
+        carry(1, 1, "vector")
+        fade_old(2)
+        deliver(3, 0, "scalar")
+        deliver(2, 1, "vector")
+        fade_old(3)
+        deliver(3, 1, "scalar")
+        finish(2, 1)
+        finish(3, 2)

@@ -39,10 +39,10 @@ def tile_attend_lookahead_delivered_lean_kernel(
             return [keep.tile(shape, dtype, name="%s%d" % (name, n), align_bytes=64) for n in range(count)]
 
         key_scales = keep.tile([P, T], U8, align_bytes=64)
-        nc.vector.memset(key_scales[:].bitcast(I32), 0)
+        scale_rows = keep.tile([P, T // 4], I32)
         for quad in range(4):
             nc.scalar.dma_start(
-                out=key_scales[32 * quad : 32 * quad + 4, :].bitcast(I32),
+                out=scale_rows[32 * quad : 32 * quad + 4, :],
                 in_=keys_scales[0, 4 * quad : 4 * quad + 4, :].bitcast(I32),
             )
         query_raw = keep.tile([P, PACK, Q], F32)
@@ -51,29 +51,34 @@ def tile_attend_lookahead_delivered_lean_kernel(
         nc.sync.dma_start(out=key_words[:].bitcast(I32), in_=keys_words[0].bitcast(I32))
         second = keep.tile([P, LIST_COLS], U16)
         nc.sync.dma_start(second[:], offs2)
-        third = keep.tile([P, LIST_COLS], U16)
-        nc.sync.dma_start(third[:], offs3)
         first = keep.tile([P, LIST_COLS], U16)
         nc.sync.dma_start(first[:], offs)
+        msgs_raw = keep.tile([P, PACK, E], F32)
+        nc.sync.dma_start(out=msgs_raw[:], in_=msgs.rearrange("(p r) e -> p r e", r=PACK))
+        third = keep.tile([P, LIST_COLS], U16)
+        nc.sync.dma_start(third[:], offs3)
+        fade_sb = keep.tile([P, 2, PACK], F32)
+        nc.sync.dma_start(out=fade_sb[:], in_=fade.rearrange("o (h p k) -> p (o h) k", h=2, k=PACK))
+        kept = tiles("kept", 4, [P, M], F32)
+        nc.sync.dma_start(out=kept[0][:], in_=old[0:P, :])
         lam_sb = keep.tile([P, PACK], F32)
         nc.sync.dma_start(out=lam_sb[:], in_=lam.rearrange("(p r) o -> p (r o)", r=PACK))
         qs_sb = keep.tile([P, PACK], F32)
         nc.sync.dma_start(out=qs_sb[:], in_=qs.rearrange("(p r) o -> p (r o)", r=PACK))
-        fade_sb = keep.tile([P, 2, PACK], F32)
-        nc.sync.dma_start(out=fade_sb[:], in_=fade.rearrange("o (h p k) -> p (o h) k", h=2, k=PACK))
-        msgs_raw = keep.tile([P, PACK, E], F32)
-        nc.sync.dma_start(out=msgs_raw[:], in_=msgs.rearrange("(p r) e -> p r e", r=PACK))
+        for et in range(1, 4):
+            nc.sync.dma_start(out=kept[et][:], in_=old[P * et : P * (et + 1), :])
         places = keep.tile([P, LIST_COLS], U16)
         nc.sync.dma_start(places[:], offs4)
-        kept = tiles("kept", 4, [P, M], F32)
-        for et in range(4):
-            nc.sync.dma_start(out=kept[et][:], in_=old[P * et : P * (et + 1), :])
 
+        nc.vector.memset(key_scales[:].bitcast(I32), 0)
         ident = keep.tile([P, P], F32)
         make_identity(nc, ident[:])
         delivered = tiles("delivered", 4, [P, M], F32)
+        for quad in range(4):
+            rows = slice(32 * quad, 32 * quad + 4)
+            nc.vector.tensor_copy(out=key_scales[rows, :].bitcast(I32), in_=scale_rows[rows, :])
         for et in range(4):
-            nc.vector.memset(delivered[et][:], 0.0)
+            (nc.vector if et < 2 else nc.gpsimd).memset(delivered[et][:], 0.0)
 
         query_bf = tiles("query_bf", PACK, [P, P, PACK], BF16)
         query_codes = tiles("query_codes", PACK, [P, P], U32)
@@ -83,8 +88,7 @@ def tile_attend_lookahead_delivered_lean_kernel(
         next_a = tiles("next_a", PACK, [P, I], F32)
         next_b = tiles("next_b", PACK, [P, I], F32)
         larger = tiles("larger", PACK, [P, I], F32)
-        weight = tiles("weight", PACK, [P, I], F32)
-        planes = tiles("planes", 2, [P, PACK, HALF], BF16)
+        weight = keep.tile([P, 2, PACK * HALF], F32)
         wq_bf = tiles("wq_bf", 2, [P, HALF, PACK], BF16)
         wq_codes = tiles("wq_codes", 2, [P, HALF], U32)
         wq_scales = tiles("wq_scales", 2, [P, HALF], U8)
@@ -136,18 +140,24 @@ def tile_attend_lookahead_delivered_lean_kernel(
             look_up(r, next_b, third, "scalar", lo, hi)
             look_up(r, own, first, own_engine, lo, hi)
 
-        def combine(r, lo, hi):
-            nc.vector.tensor_tensor(larger[r][:, lo:hi], next_a[r][:, lo:hi], next_b[r][:, lo:hi], MAX)
+        def combine(r, lo, hi, scratch):
+            nc.vector.tensor_tensor(scratch, next_a[r][:, lo:hi], next_b[r][:, lo:hi], MAX)
             nc.vector.scalar_tensor_tensor(
-                weight[r][:, lo:hi], larger[r][:, lo:hi], lam_sb[:, r : r + 1], own[r][:, lo:hi], MULT, ADD
+                weight[:, lo // HALF : hi // HALF, HALF * r : HALF * (r + 1)],
+                scratch.rearrange("p (h i) -> p h i", i=HALF),
+                lam_sb[:, r : r + 1],
+                own[r][:, lo:hi].rearrange("p (h i) -> p h i", i=HALF),
+                MULT,
+                ADD,
             )
-            for h in range(lo // HALF, hi // HALF):
-                nc.vector.tensor_scalar(
-                    planes[h][:, r, :], weight[r][:, HALF * h : HALF * (h + 1)], qs_sb[:, r : r + 1], None, MULT
-                )
 
         def quantize_weights(h):
-            nc.vector.tensor_copy(out=wq_bf[h][:], in_=planes[h][:].rearrange("p r i -> p i r"))
+            nc.vector.tensor_tensor(
+                wq_bf[h][:].rearrange("p (c i) r -> p c r i", i=4),
+                weight[:, h, :].rearrange("p (r c i) -> p c r i", r=PACK, i=4),
+                qs_sb[:].unsqueeze(1).unsqueeze(3).to_broadcast([P, HALF // 4, PACK, 4]),
+                MULT,
+            )
             quantize(wq_codes[h], wq_scales[h], wq_bf[h])
 
         def carry(h, pair, engine):
@@ -177,64 +187,69 @@ def tile_attend_lookahead_delivered_lean_kernel(
             else:
                 nc.scalar.activation(window, src, COPY)
 
-        def fade_old(et):
+        def fade_old(et, dst):
             for h in range(2):
-                part = kept[et][:, BANK * h : BANK * (h + 1)].rearrange("p (n k) -> p n k", k=PACK)
-                nc.vector.tensor_tensor(part, part, fade_rows[h][:].rearrange("p k n -> p n k"), MULT)
+                cols = slice(BANK * h, BANK * (h + 1))
+                nc.vector.tensor_tensor(
+                    dst[:, cols].rearrange("p (n k) -> p n k", k=PACK),
+                    kept[et][:, cols].rearrange("p (n k) -> p n k", k=PACK),
+                    fade_rows[h][:].rearrange("p k n -> p n k"),
+                    MULT,
+                )
 
-        def finish(et, pieces):
+        def finish(et, faded, pieces):
             width = M // pieces
             for n in range(pieces):
                 cols = slice(width * n, width * (n + 1))
-                nc.vector.tensor_tensor(kept[et][:, cols], kept[et][:, cols], delivered[et][:, cols], ADD)
+                nc.vector.tensor_tensor(kept[et][:, cols], faded[:, cols], delivered[et][:, cols], ADD)
                 nc.sync.dma_start(out=out[P * et : P * (et + 1), cols], in_=kept[et][:, cols])
 
         lay_query(0, "vector")
         lay_query(1, "scalar")
         quantize(query_codes[0], query_scales[0], query_bf[0])
         lay_query(2, "vector")
+        lay_query(3, "scalar")
         quantize(query_codes[1], query_scales[1], query_bf[1])
         score(0, ("vector", "scalar"))
         look_up_all(0, 0, I, "vector")
-        lay_query(3, "vector")
         quantize(query_codes[2], query_scales[2], query_bf[2])
         quantize(query_codes[3], query_scales[3], query_bf[3])
-        score(1, ("scalar", "scalar"))
+        score(1, ("vector", "scalar"))
         for h in range(2):
             for k in range(PACK):
                 nc.tensor.transpose(fade_rows[h][:, k, :], fade_sb[:, h, k : k + 1].to_broadcast([P, P]), ident[:])
-        combine(0, 0, I)
+        combine(0, 0, I, larger[0][:])
         look_up_all(1, 0, I, "vector")
-        score(2, ("scalar", "scalar"))
+        score(2, ("vector", "scalar"))
         nc.vector.tensor_copy(out=msgs_bf[:], in_=msgs_raw[:].rearrange("p r e -> p e r"))
-        combine(1, 0, I)
+        fade_old(0, kept[0][:])
         quantize(msgs_codes, msgs_scales, msgs_bf)
-        look_up_all(2, 0, I, "vector")
-        score(3, ("scalar", "scalar"))
-        fade_old(0)
-        combine(2, 0, I)
-        look_up_all(3, 0, HALF, "vector")
-        fade_old(1)
-        combine(3, 0, HALF)
+        combine(1, 0, I, larger[1][:])
+        look_up_all(2, 0, I, "scalar")
+        score(3, ("vector", "scalar"))
+        fade_old(1, kept[1][:])
+        fade_old(2, kept[2][:])
+        combine(2, 0, I, larger[2][:])
+        look_up_all(3, 0, HALF, "scalar")
+        combine(3, 0, HALF, larger[3][:, 0:HALF])
         look_up_all(3, HALF, I, "scalar")
         quantize_weights(0)
         carry(0, 0, "scalar")
         deliver(0, 0, "scalar")
         deliver(1, 0, "scalar")
-        combine(3, HALF, I)
+        combine(3, HALF, I, weight[:, 0, 0:HALF])
         quantize_weights(1)
-        carry(1, 0, "vector")
-        deliver(0, 1, "vector")
-        deliver(1, 1, "scalar")
-        finish(0, 1)
+        fade_old(3, weight[:, 1, :])
         carry(0, 1, "scalar")
+        carry(1, 0, "vector")
         deliver(2, 0, "scalar")
-        finish(1, 1)
-        carry(1, 1, "vector")
-        fade_old(2)
         deliver(3, 0, "scalar")
-        deliver(2, 1, "vector")
-        fade_old(3)
+        deliver(0, 1, "vector")
+        finish(0, kept[0][:], 1)
+        carry(1, 1, "vector")
+        deliver(1, 1, "vector")
+        deliver(2, 1, "scalar")
+        finish(1, kept[1][:], 1)
         deliver(3, 1, "scalar")
-        finish(2, 1)
-        finish(3, 2)
+        finish(2, kept[2][:], 1)
+        finish(3, weight[:, 1, :], 2)

@@ -1,7 +1,6 @@
 from contextlib import ExitStack
 
 import concourse.mybir as mybir
-from concourse.masks import make_identity
 
 D, T, I, Q, E, M = 512, 1024, 512, 512, 512, 1024
 FLOPS = 2 * D * Q * T + 2 * Q * E * I
@@ -32,17 +31,15 @@ def tile_attend_lookahead_delivered_lean_kernel(
     nc = tc.nc
     with ExitStack() as ctx:
         keep = ctx.enter_context(tc.tile_pool(name="keep", bufs=1))
-        psum_fade = ctx.enter_context(tc.psum_pool(name="psum_fade", bufs=1))
-        psum = ctx.enter_context(tc.psum_pool(name="psum", bufs=6))
+        psum = ctx.enter_context(tc.psum_pool(name="psum", bufs=8))
 
         def tiles(name, count, shape, dtype):
             return [keep.tile(shape, dtype, name="%s%d" % (name, n), align_bytes=64) for n in range(count)]
 
         key_scales = keep.tile([P, T], U8, align_bytes=64)
-        scale_rows = keep.tile([P, T // 4], I32)
         for quad in range(4):
             nc.scalar.dma_start(
-                out=scale_rows[32 * quad : 32 * quad + 4, :],
+                out=key_scales[32 * quad : 32 * quad + 4, :].bitcast(I32),
                 in_=keys_scales[0, 4 * quad : 4 * quad + 4, :].bitcast(I32),
             )
         query_raw = keep.tile([P, PACK, Q], F32)
@@ -57,30 +54,25 @@ def tile_attend_lookahead_delivered_lean_kernel(
         nc.sync.dma_start(out=msgs_raw[:], in_=msgs.rearrange("(p r) e -> p r e", r=PACK))
         third = keep.tile([P, LIST_COLS], U16)
         nc.sync.dma_start(third[:], offs3)
-        fade_sb = keep.tile([P, 2, PACK], F32)
-        nc.sync.dma_start(out=fade_sb[:], in_=fade.rearrange("o (h p k) -> p (o h) k", h=2, k=PACK))
         kept = tiles("kept", 4, [P, M], F32)
         nc.sync.dma_start(out=kept[0][:], in_=old[0:P, :])
         lam_sb = keep.tile([P, PACK], F32)
         nc.sync.dma_start(out=lam_sb[:], in_=lam.rearrange("(p r) o -> p (r o)", r=PACK))
         qs_sb = keep.tile([P, PACK], F32)
         nc.sync.dma_start(out=qs_sb[:], in_=qs.rearrange("(p r) o -> p (r o)", r=PACK))
+        fade_rows = keep.tile([P, M], F32)
+        nc.sync.dma_start(out=fade_rows[:], in_=fade[0].partition_broadcast(P))
         for et in range(1, 4):
             nc.sync.dma_start(out=kept[et][:], in_=old[P * et : P * (et + 1), :])
         places = keep.tile([P, LIST_COLS], U16)
         nc.sync.dma_start(places[:], offs4)
 
-        nc.vector.memset(key_scales[:].bitcast(I32), 0)
-        ident = keep.tile([P, P], F32)
-        make_identity(nc, ident[:])
         delivered = tiles("delivered", 4, [P, M], F32)
-        for quad in range(4):
-            rows = slice(32 * quad, 32 * quad + 4)
-            nc.vector.tensor_copy(out=key_scales[rows, :].bitcast(I32), in_=scale_rows[rows, :])
         for et in range(4):
             (nc.vector if et < 2 else nc.gpsimd).memset(delivered[et][:], 0.0)
 
-        query_bf = tiles("query_bf", PACK, [P, P, PACK], BF16)
+        laid = keep.tile([P, E * PACK], BF16, align_bytes=64)
+        query_bf = [laid[:, P * PACK * n : P * PACK * (n + 1)] for n in (0, 1, 0, 2)]
         query_codes = tiles("query_codes", PACK, [P, P], U32)
         query_scales = tiles("query_scales", PACK, [P, P], U8)
         scores = tiles("scores", PACK, [P, T], F32)
@@ -89,25 +81,23 @@ def tile_attend_lookahead_delivered_lean_kernel(
         next_b = tiles("next_b", PACK, [P, I], F32)
         larger = tiles("larger", PACK, [P, I], F32)
         weight = keep.tile([P, 2, PACK * HALF], F32)
-        wq_bf = tiles("wq_bf", 2, [P, HALF, PACK], BF16)
+        wq_bf = keep.tile([P, 2 * HALF * PACK], BF16, align_bytes=64)
         wq_codes = tiles("wq_codes", 2, [P, HALF], U32)
         wq_scales = tiles("wq_scales", 2, [P, HALF], U8)
-        msgs_bf = keep.tile([P, E, PACK], BF16, align_bytes=64)
         msgs_codes = keep.tile([P, E], U32, align_bytes=64)
         msgs_scales = keep.tile([P, E], U8, align_bytes=64)
         sums = tiles("sums", 4, [P, 2, HALF], F32)
-        fade_rows = [psum_fade.tile([P, PACK, P], F32, name="fade_rows%d" % h) for h in range(2)]
 
         def lay_query(r, engine):
             src = query_raw[:].rearrange("p j (s r) -> p r s j", r=PACK)[:, r]
             if engine == "vector":
-                nc.vector.tensor_copy(out=query_bf[r][:], in_=src)
+                nc.vector.tensor_copy(out=query_bf[r].rearrange("p (s j) -> p s j", j=PACK), in_=src)
             else:
-                nc.scalar.copy(out=query_bf[r][:], in_=src)
+                nc.scalar.copy(out=query_bf[r].rearrange("p (s j) -> p s j", j=PACK), in_=src)
 
         def quantize(codes, scales, values):
             nc.vector.quantize_mx(
-                out=codes[:].bitcast(FP8X4), scales=scales[:], in_=values[:].rearrange("p n j -> p (n j)")
+                out=codes[:].bitcast(FP8X4), scales=scales[:], in_=values
             )
 
         def score(r, engines):
@@ -135,9 +125,9 @@ def tile_attend_lookahead_delivered_lean_kernel(
             else:
                 nc.scalar.activation(dst[r][:, lo:hi], window, COPY)
 
-        def look_up_all(r, lo, hi, own_engine):
+        def look_up_all(r, lo, hi, own_engine, third_engine="scalar"):
             look_up(r, next_a, second, "scalar", lo, hi)
-            look_up(r, next_b, third, "scalar", lo, hi)
+            look_up(r, next_b, third, third_engine, lo, hi)
             look_up(r, own, first, own_engine, lo, hi)
 
         def combine(r, lo, hi, scratch):
@@ -153,12 +143,12 @@ def tile_attend_lookahead_delivered_lean_kernel(
 
         def quantize_weights(h):
             nc.vector.tensor_tensor(
-                wq_bf[h][:].rearrange("p (c i) r -> p c r i", i=4),
+                wq_bf[:, HALF * PACK * h : HALF * PACK * (h + 1)].rearrange("p (c i r) -> p c r i", i=4, r=PACK),
                 weight[:, h, :].rearrange("p (r c i) -> p c r i", r=PACK, i=4),
                 qs_sb[:].unsqueeze(1).unsqueeze(3).to_broadcast([P, HALF // 4, PACK, 4]),
                 MULT,
             )
-            quantize(wq_codes[h], wq_scales[h], wq_bf[h])
+            quantize(wq_codes[h], wq_scales[h], wq_bf[:, HALF * PACK * h : HALF * PACK * (h + 1)])
 
         def carry(h, pair, engine):
             bank = psum.tile([P, 2, HALF], F32, name="bank")
@@ -187,22 +177,15 @@ def tile_attend_lookahead_delivered_lean_kernel(
             else:
                 nc.scalar.activation(window, src, COPY)
 
-        def fade_old(et, dst):
-            for h in range(2):
-                cols = slice(BANK * h, BANK * (h + 1))
-                nc.vector.tensor_tensor(
-                    dst[:, cols].rearrange("p (n k) -> p n k", k=PACK),
-                    kept[et][:, cols].rearrange("p (n k) -> p n k", k=PACK),
-                    fade_rows[h][:].rearrange("p k n -> p n k"),
-                    MULT,
-                )
+        def fade_old(et, dst, engine):
+            engine.tensor_tensor(dst, kept[et][:], fade_rows[:], MULT)
 
         def finish(et, faded, pieces):
             width = M // pieces
             for n in range(pieces):
                 cols = slice(width * n, width * (n + 1))
-                nc.vector.tensor_tensor(kept[et][:, cols], faded[:, cols], delivered[et][:, cols], ADD)
-                nc.sync.dma_start(out=out[P * et : P * (et + 1), cols], in_=kept[et][:, cols])
+                nc.vector.tensor_tensor(faded[:, cols], faded[:, cols], delivered[et][:, cols], ADD)
+                nc.sync.dma_start(out=out[P * et : P * (et + 1), cols], in_=faded[:, cols])
 
         lay_query(0, "vector")
         lay_query(1, "scalar")
@@ -211,35 +194,36 @@ def tile_attend_lookahead_delivered_lean_kernel(
         lay_query(3, "scalar")
         quantize(query_codes[1], query_scales[1], query_bf[1])
         score(0, ("vector", "scalar"))
-        look_up_all(0, 0, I, "vector")
+        look_up_all(0, 0, I, "vector", "vector")
         quantize(query_codes[2], query_scales[2], query_bf[2])
         quantize(query_codes[3], query_scales[3], query_bf[3])
-        score(1, ("vector", "scalar"))
-        for h in range(2):
-            for k in range(PACK):
-                nc.tensor.transpose(fade_rows[h][:, k, :], fade_sb[:, h, k : k + 1].to_broadcast([P, P]), ident[:])
+        score(1, ("scalar", "scalar"))
         combine(0, 0, I, larger[0][:])
         look_up_all(1, 0, I, "vector")
-        score(2, ("vector", "scalar"))
-        nc.vector.tensor_copy(out=msgs_bf[:], in_=msgs_raw[:].rearrange("p r e -> p e r"))
-        fade_old(0, kept[0][:])
-        quantize(msgs_codes, msgs_scales, msgs_bf)
-        combine(1, 0, I, larger[1][:])
-        look_up_all(2, 0, I, "scalar")
+        score(2, ("scalar", "scalar"))
         score(3, ("vector", "scalar"))
-        fade_old(1, kept[1][:])
-        fade_old(2, kept[2][:])
-        combine(2, 0, I, larger[2][:])
-        look_up_all(3, 0, HALF, "scalar")
+        nc.gpsimd.tensor_scalar(
+            laid[:].rearrange("p (e r) -> p e r", r=PACK), msgs_raw[:].rearrange("p r e -> p e r"), 1.0, 0.0, MULT, ADD
+        )
+        quantize(msgs_codes, msgs_scales, laid[:])
+        combine(1, 0, I, larger[1][:])
+        look_up_all(2, 0, HALF, "vector")
+        look_up_all(3, 0, HALF, "vector")
+        fade_old(0, kept[0][:], nc.vector)
+        combine(2, 0, HALF, larger[2][:, 0:HALF])
         combine(3, 0, HALF, larger[3][:, 0:HALF])
+        look_up_all(2, HALF, I, "scalar")
         look_up_all(3, HALF, I, "scalar")
         quantize_weights(0)
         carry(0, 0, "scalar")
         deliver(0, 0, "scalar")
         deliver(1, 0, "scalar")
-        combine(3, HALF, I, weight[:, 0, 0:HALF])
+        combine(2, HALF, I, weight[:, 0, 0:HALF])
+        combine(3, HALF, I, weight[:, 0, HALF : 2 * HALF])
         quantize_weights(1)
-        fade_old(3, weight[:, 1, :])
+        fade_old(1, wq_bf[:].bitcast(F32), nc.vector)
+        fade_old(2, kept[1][:], nc.gpsimd)
+        fade_old(3, kept[2][:], nc.gpsimd)
         carry(0, 1, "scalar")
         carry(1, 0, "vector")
         deliver(2, 0, "scalar")
@@ -249,7 +233,7 @@ def tile_attend_lookahead_delivered_lean_kernel(
         carry(1, 1, "vector")
         deliver(1, 1, "vector")
         deliver(2, 1, "scalar")
-        finish(1, kept[1][:], 1)
+        finish(1, wq_bf[:].bitcast(F32), 1)
         deliver(3, 1, "scalar")
-        finish(2, kept[2][:], 1)
-        finish(3, weight[:, 1, :], 2)
+        finish(2, kept[1][:], 1)
+        finish(3, kept[2][:], 2)

@@ -82,11 +82,11 @@ def tile_attend_lookahead_delivered_lean_kernel(
         larger = tiles("larger", PACK, [P, I], F32)
         weight = keep.tile([P, 2, PACK * HALF], F32)
         wq_bf = keep.tile([P, 2 * HALF * PACK], BF16, align_bytes=64)
-        wq_codes = tiles("wq_codes", 2, [P, HALF], U32)
-        wq_scales = tiles("wq_scales", 2, [P, HALF], U8)
+        wq_codes = keep.tile([P, I], U32, align_bytes=64)
+        wq_scales = keep.tile([P, I], U8, align_bytes=64)
         msgs_codes = keep.tile([P, E], U32, align_bytes=64)
         msgs_scales = keep.tile([P, E], U8, align_bytes=64)
-        sums = tiles("sums", 4, [P, 2, HALF], F32)
+        sums = tiles("sums", 4, [P, I], F32)
 
         def lay_query(r, engine):
             src = query_raw[:].rearrange("p j (s r) -> p r s j", r=PACK)[:, r]
@@ -97,7 +97,7 @@ def tile_attend_lookahead_delivered_lean_kernel(
 
         def quantize(codes, scales, values):
             nc.vector.quantize_mx(
-                out=codes[:].bitcast(FP8X4), scales=scales[:], in_=values
+                out=codes.bitcast(FP8X4), scales=scales, in_=values
             )
 
         def score(r, engines):
@@ -148,30 +148,30 @@ def tile_attend_lookahead_delivered_lean_kernel(
                 qs_sb[:].unsqueeze(1).unsqueeze(3).to_broadcast([P, HALF // 4, PACK, 4]),
                 MULT,
             )
-            quantize(wq_codes[h], wq_scales[h], wq_bf[:, HALF * PACK * h : HALF * PACK * (h + 1)])
+            quantize(wq_codes[:, HALF * h : HALF * (h + 1)], wq_scales[:, HALF * h : HALF * (h + 1)], wq_bf[:, HALF * PACK * h : HALF * PACK * (h + 1)])
 
-        def carry(h, pair, engine):
-            bank = psum.tile([P, 2, HALF], F32, name="bank")
-            for n in range(2):
-                cols = slice(P * (2 * pair + n), P * (2 * pair + n + 1))
+        def carry(dst, parts, engine):
+            bank = psum.tile([P, BANK], F32, name="bank")
+            at = 0
+            for et, lo, hi in parts:
+                cols = slice(P * et, P * (et + 1))
                 nc.tensor.matmul_mx(
-                    out=bank[:, n, :],
+                    out=bank[:, at : at + hi - lo],
                     lhsT=msgs_codes[:, cols].bitcast(FP8X4),
                     lhsT_scale=msgs_scales[:, cols],
-                    rhs=wq_codes[h][:].bitcast(FP8X4),
-                    rhs_scale=wq_scales[h][:],
+                    rhs=wq_codes[:, lo:hi].bitcast(FP8X4),
+                    rhs_scale=wq_scales[:, lo:hi],
                     start=True,
                     stop=True,
                 )
-            dst = sums[2 * h + pair][:]
+                at = at + hi - lo
             if engine == "vector":
-                nc.vector.tensor_copy(out=dst, in_=bank[:])
+                nc.vector.tensor_copy(out=dst[:], in_=bank[:])
             else:
-                nc.scalar.copy(out=dst, in_=bank[:])
+                nc.scalar.copy(out=dst[:], in_=bank[:])
 
-        def deliver(et, h, engine):
-            window = delivered[et][:].indirect(places[:, HALF * h // 16 : HALF * (h + 1) // 16])
-            src = sums[2 * h + et // 2][:, et % 2, :]
+        def deliver(et, lo, hi, src, engine):
+            window = delivered[et][:].indirect(places[:, lo // 16 : hi // 16])
             if engine == "vector":
                 nc.vector.tensor_copy(window, src)
             else:
@@ -189,51 +189,50 @@ def tile_attend_lookahead_delivered_lean_kernel(
 
         lay_query(0, "vector")
         lay_query(1, "scalar")
-        quantize(query_codes[0], query_scales[0], query_bf[0])
+        quantize(query_codes[0][:], query_scales[0][:], query_bf[0])
         lay_query(2, "vector")
         lay_query(3, "scalar")
-        quantize(query_codes[1], query_scales[1], query_bf[1])
+        quantize(query_codes[1][:], query_scales[1][:], query_bf[1])
         score(0, ("vector", "scalar"))
         look_up_all(0, 0, I, "vector", "vector")
-        quantize(query_codes[2], query_scales[2], query_bf[2])
-        quantize(query_codes[3], query_scales[3], query_bf[3])
+        quantize(query_codes[2][:], query_scales[2][:], query_bf[2])
+        quantize(query_codes[3][:], query_scales[3][:], query_bf[3])
         score(1, ("scalar", "scalar"))
         combine(0, 0, I, larger[0][:])
-        look_up_all(1, 0, I, "vector")
-        score(2, ("scalar", "scalar"))
-        score(3, ("vector", "scalar"))
+        look_up_all(1, 0, I, "vector", "vector")
+        score(2, ("vector", "scalar"))
+        score(3, ("scalar", "scalar"))
         nc.gpsimd.tensor_scalar(
             laid[:].rearrange("p (e r) -> p e r", r=PACK), msgs_raw[:].rearrange("p r e -> p e r"), 1.0, 0.0, MULT, ADD
         )
-        quantize(msgs_codes, msgs_scales, laid[:])
+        quantize(msgs_codes[:], msgs_scales[:], laid[:])
         combine(1, 0, I, larger[1][:])
-        look_up_all(2, 0, HALF, "vector")
-        look_up_all(3, 0, HALF, "vector")
+        look_up_all(2, 0, HALF, "scalar")
+        look_up_all(3, 0, HALF, "scalar")
         fade_old(0, kept[0][:], nc.vector)
         combine(2, 0, HALF, larger[2][:, 0:HALF])
         combine(3, 0, HALF, larger[3][:, 0:HALF])
         look_up_all(2, HALF, I, "scalar")
         look_up_all(3, HALF, I, "scalar")
         quantize_weights(0)
-        carry(0, 0, "scalar")
-        deliver(0, 0, "scalar")
-        deliver(1, 0, "scalar")
+        carry(sums[0], [(0, 0, HALF), (1, 0, HALF)], "scalar")
+        deliver(0, 0, HALF, sums[0][:, 0:HALF], "scalar")
+        deliver(1, 0, HALF, sums[0][:, HALF:I], "scalar")
         combine(2, HALF, I, weight[:, 0, 0:HALF])
         combine(3, HALF, I, weight[:, 0, HALF : 2 * HALF])
         quantize_weights(1)
-        fade_old(1, wq_bf[:].bitcast(F32), nc.vector)
+        fade_old(1, wq_bf[:].bitcast(F32), nc.gpsimd)
         fade_old(2, kept[1][:], nc.gpsimd)
-        fade_old(3, kept[2][:], nc.gpsimd)
-        carry(0, 1, "scalar")
-        carry(1, 0, "vector")
-        deliver(2, 0, "scalar")
-        deliver(3, 0, "scalar")
-        deliver(0, 1, "vector")
+        carry(sums[2], [(2, 0, I)], "vector")
+        deliver(2, 0, I, sums[2][:], "vector")
+        carry(sums[1], [(0, HALF, I), (1, HALF, I)], "scalar")
+        deliver(0, HALF, I, sums[1][:, 0:HALF], "scalar")
+        deliver(1, HALF, I, sums[1][:, HALF:I], "scalar")
+        carry(sums[3], [(3, 0, I)], "scalar")
+        deliver(3, 0, HALF, sums[3][:, 0:HALF], "scalar")
+        deliver(3, HALF, I, sums[3][:, HALF:I], "scalar")
         finish(0, kept[0][:], 1)
-        carry(1, 1, "vector")
-        deliver(1, 1, "vector")
-        deliver(2, 1, "scalar")
         finish(1, wq_bf[:].bitcast(F32), 1)
-        deliver(3, 1, "scalar")
         finish(2, kept[1][:], 1)
+        fade_old(3, kept[2][:], nc.vector)
         finish(3, kept[2][:], 2)

@@ -21,23 +21,29 @@ COPY = mybir.ActivationFunctionType.Copy
 P = 128
 PACK = 4
 BANK = 512
+BANKS = 8
+E_TILES = E // P
+QUADS = 4
+PER_COL = 16
+LINE = 4
 HALF = I // 2
-LIST_COLS = I // 16
+LAST_PIECES = 2
 
 
 def tile_attend_lookahead_delivered_lean_kernel(
     tc, query, keys_words, keys_scales, lam, qs, msgs, old, fade, offs, offs2, offs3, offs4, out
 ):
     nc = tc.nc
+    vector, scalar, gpsimd = nc.vector, nc.scalar, nc.gpsimd
     with ExitStack() as ctx:
         keep = ctx.enter_context(tc.tile_pool(name="keep", bufs=1))
-        psum = ctx.enter_context(tc.psum_pool(name="psum", bufs=8))
+        psum = ctx.enter_context(tc.psum_pool(name="psum", bufs=BANKS))
 
         def tiles(name, count, shape, dtype):
             return [keep.tile(shape, dtype, name="%s%d" % (name, n), align_bytes=64) for n in range(count)]
 
         key_scales = keep.tile([P, T], U8, align_bytes=64)
-        for quad in range(4):
+        for quad in range(QUADS):
             nc.scalar.dma_start(
                 out=key_scales[32 * quad : 32 * quad + 4, :].bitcast(I32),
                 in_=keys_scales[0, 4 * quad : 4 * quad + 4, :].bitcast(I32),
@@ -46,15 +52,15 @@ def tile_attend_lookahead_delivered_lean_kernel(
         nc.sync.dma_start(out=query_raw[:], in_=query.rearrange("(p j) q -> p j q", j=PACK))
         key_words = keep.tile([P, 2 * T], U8, align_bytes=64)
         nc.sync.dma_start(out=key_words[:].bitcast(I32), in_=keys_words[0].bitcast(I32))
-        second = keep.tile([P, LIST_COLS], U16)
+        second = keep.tile([P, I // PER_COL], U16)
         nc.sync.dma_start(second[:], offs2)
-        first = keep.tile([P, LIST_COLS], U16)
+        first = keep.tile([P, I // PER_COL], U16)
         nc.sync.dma_start(first[:], offs)
         msgs_raw = keep.tile([P, PACK, E], F32)
         nc.sync.dma_start(out=msgs_raw[:], in_=msgs.rearrange("(p r) e -> p r e", r=PACK))
-        third = keep.tile([P, LIST_COLS], U16)
+        third = keep.tile([P, I // PER_COL], U16)
         nc.sync.dma_start(third[:], offs3)
-        kept = tiles("kept", 4, [P, M], F32)
+        kept = tiles("kept", E_TILES, [P, M], F32)
         nc.sync.dma_start(out=kept[0][:], in_=old[0:P, :])
         lam_sb = keep.tile([P, PACK], F32)
         nc.sync.dma_start(out=lam_sb[:], in_=lam.rearrange("(p r) o -> p (r o)", r=PACK))
@@ -62,17 +68,17 @@ def tile_attend_lookahead_delivered_lean_kernel(
         nc.sync.dma_start(out=qs_sb[:], in_=qs.rearrange("(p r) o -> p (r o)", r=PACK))
         fade_rows = keep.tile([P, M], F32)
         nc.sync.dma_start(out=fade_rows[:], in_=fade[0].partition_broadcast(P))
-        for et in range(1, 4):
+        for et in range(1, E_TILES):
             nc.sync.dma_start(out=kept[et][:], in_=old[P * et : P * (et + 1), :])
-        places = keep.tile([P, LIST_COLS], U16)
+        places = keep.tile([P, I // PER_COL], U16)
         nc.sync.dma_start(places[:], offs4)
 
-        delivered = tiles("delivered", 4, [P, M], F32)
-        for et in range(4):
-            (nc.vector if et < 2 else nc.gpsimd).memset(delivered[et][:], 0.0)
+        delivered = tiles("delivered", E_TILES, [P, M], F32)
+        for et in range(E_TILES):
+            (vector if et < E_TILES // 2 else gpsimd).memset(delivered[et][:], 0.0)
 
         laid = keep.tile([P, E * PACK], BF16, align_bytes=64)
-        query_bf = [laid[:, P * PACK * n : P * PACK * (n + 1)] for n in (0, 1, 0, 2)]
+        query_bf = [laid[:, P * PACK * place : P * PACK * (place + 1)] for place in (0, 1, 0, 2)]
         query_codes = tiles("query_codes", PACK, [P, P], U32)
         query_scales = tiles("query_scales", PACK, [P, P], U8)
         scores = tiles("scores", PACK, [P, T], F32)
@@ -81,58 +87,56 @@ def tile_attend_lookahead_delivered_lean_kernel(
         next_b = tiles("next_b", PACK, [P, I], F32)
         larger = tiles("larger", PACK, [P, I], F32)
         weight = keep.tile([P, 2, PACK * HALF], F32)
-        wq_bf = keep.tile([P, 2 * HALF * PACK], BF16, align_bytes=64)
+        wq_bf = keep.tile([P, I * PACK], BF16, align_bytes=64)
         wq_codes = keep.tile([P, I], U32, align_bytes=64)
         wq_scales = keep.tile([P, I], U8, align_bytes=64)
         msgs_codes = keep.tile([P, E], U32, align_bytes=64)
         msgs_scales = keep.tile([P, E], U8, align_bytes=64)
-        sums = tiles("sums", 4, [P, I], F32)
+        sums = tiles("sums", E_TILES, [P, I], F32)
+
+        def copy(engine, dst, src):
+            if engine is vector:
+                vector.tensor_copy(out=dst, in_=src)
+            else:
+                scalar.copy(out=dst, in_=src)
+
+        def copy_listed(engine, dst, src):
+            if engine is vector:
+                vector.tensor_copy(dst, src)
+            else:
+                scalar.activation(dst, src, COPY)
+
+        def quantize(codes, scales, values):
+            vector.quantize_mx(out=codes.bitcast(FP8X4), scales=scales, in_=values)
 
         def lay_query(r, engine):
             src = query_raw[:].rearrange("p j (s r) -> p r s j", r=PACK)[:, r]
-            if engine == "vector":
-                nc.vector.tensor_copy(out=query_bf[r].rearrange("p (s j) -> p s j", j=PACK), in_=src)
-            else:
-                nc.scalar.copy(out=query_bf[r].rearrange("p (s j) -> p s j", j=PACK), in_=src)
+            copy(engine, query_bf[r].rearrange("p (s j) -> p s j", j=PACK), src)
 
-        def quantize(codes, scales, values):
-            nc.vector.quantize_mx(
-                out=codes.bitcast(FP8X4), scales=scales, in_=values
-            )
+        def quantize_query(r):
+            quantize(query_codes[r][:], query_scales[r][:], query_bf[r])
 
         def score(r, engines):
-            for h in range(2):
+            for n, engine in enumerate(engines):
                 bank = psum.tile([P, BANK], F32, name="bank")
                 nc.tensor.matmul_mx(
                     out=bank[:],
                     lhsT=query_codes[r][:].bitcast(FP8X4),
                     lhsT_scale=query_scales[r][:],
-                    rhs=key_words[:, 2 * BANK * h : 2 * BANK * (h + 1)].bitcast(FP4X4),
-                    rhs_scale=key_scales[:, BANK * h : BANK * (h + 1)],
+                    rhs=key_words[:, 2 * BANK * n : 2 * BANK * (n + 1)].bitcast(FP4X4),
+                    rhs_scale=key_scales[:, BANK * n : BANK * (n + 1)],
                     start=True,
                     stop=True,
                 )
-                dst = scores[r][:, BANK * h : BANK * (h + 1)]
-                if engines[h] == "vector":
-                    nc.vector.tensor_copy(out=dst, in_=bank[:])
-                else:
-                    nc.scalar.copy(out=dst, in_=bank[:])
+                copy(engine, scores[r][:, BANK * n : BANK * (n + 1)], bank[:])
 
-        def look_up(r, dst, offsets, engine, lo, hi):
-            window = scores[r][:].indirect(offsets[:, lo // 16 : hi // 16])
-            if engine == "vector":
-                nc.vector.tensor_copy(dst[r][:, lo:hi], window)
-            else:
-                nc.scalar.activation(dst[r][:, lo:hi], window, COPY)
-
-        def look_up_all(r, lo, hi, own_engine, third_engine="scalar"):
-            look_up(r, next_a, second, "scalar", lo, hi)
-            look_up(r, next_b, third, third_engine, lo, hi)
-            look_up(r, own, first, own_engine, lo, hi)
+        def look_up(r, lo, hi, engine):
+            for dst, offsets, by in ((next_a, second, scalar), (next_b, third, engine), (own, first, engine)):
+                copy_listed(by, dst[r][:, lo:hi], scores[r][:].indirect(offsets[:, lo // PER_COL : hi // PER_COL]))
 
         def combine(r, lo, hi, scratch):
-            nc.vector.tensor_tensor(scratch, next_a[r][:, lo:hi], next_b[r][:, lo:hi], MAX)
-            nc.vector.scalar_tensor_tensor(
+            vector.tensor_tensor(scratch, next_a[r][:, lo:hi], next_b[r][:, lo:hi], MAX)
+            vector.scalar_tensor_tensor(
                 weight[:, lo // HALF : hi // HALF, HALF * r : HALF * (r + 1)],
                 scratch.rearrange("p (h i) -> p h i", i=HALF),
                 lam_sb[:, r : r + 1],
@@ -142,21 +146,22 @@ def tile_attend_lookahead_delivered_lean_kernel(
             )
 
         def quantize_weights(h):
-            nc.vector.tensor_tensor(
-                wq_bf[:, HALF * PACK * h : HALF * PACK * (h + 1)].rearrange("p (c i r) -> p c r i", i=4, r=PACK),
-                weight[:, h, :].rearrange("p (r c i) -> p c r i", r=PACK, i=4),
-                qs_sb[:].unsqueeze(1).unsqueeze(3).to_broadcast([P, HALF // 4, PACK, 4]),
+            values = wq_bf[:, HALF * PACK * h : HALF * PACK * (h + 1)]
+            vector.tensor_tensor(
+                values.rearrange("p (c i r) -> p c r i", i=LINE, r=PACK),
+                weight[:, h, :].rearrange("p (r c i) -> p c r i", r=PACK, i=LINE),
+                qs_sb[:].unsqueeze(1).unsqueeze(3).to_broadcast([P, HALF // LINE, PACK, LINE]),
                 MULT,
             )
-            quantize(wq_codes[:, HALF * h : HALF * (h + 1)], wq_scales[:, HALF * h : HALF * (h + 1)], wq_bf[:, HALF * PACK * h : HALF * PACK * (h + 1)])
+            quantize(wq_codes[:, HALF * h : HALF * (h + 1)], wq_scales[:, HALF * h : HALF * (h + 1)], values)
 
         def carry(dst, parts, engine):
             bank = psum.tile([P, BANK], F32, name="bank")
-            at = 0
+            filled = 0
             for et, lo, hi in parts:
                 cols = slice(P * et, P * (et + 1))
                 nc.tensor.matmul_mx(
-                    out=bank[:, at : at + hi - lo],
+                    out=bank[:, filled : filled + hi - lo],
                     lhsT=msgs_codes[:, cols].bitcast(FP8X4),
                     lhsT_scale=msgs_scales[:, cols],
                     rhs=wq_codes[:, lo:hi].bitcast(FP8X4),
@@ -164,18 +169,11 @@ def tile_attend_lookahead_delivered_lean_kernel(
                     start=True,
                     stop=True,
                 )
-                at = at + hi - lo
-            if engine == "vector":
-                nc.vector.tensor_copy(out=dst[:], in_=bank[:])
-            else:
-                nc.scalar.copy(out=dst[:], in_=bank[:])
+                filled = filled + hi - lo
+            copy(engine, dst, bank[:, 0:filled])
 
         def deliver(et, lo, hi, src, engine):
-            window = delivered[et][:].indirect(places[:, lo // 16 : hi // 16])
-            if engine == "vector":
-                nc.vector.tensor_copy(window, src)
-            else:
-                nc.scalar.activation(window, src, COPY)
+            copy_listed(engine, delivered[et][:].indirect(places[:, lo // PER_COL : hi // PER_COL]), src)
 
         def fade_old(et, dst, engine):
             engine.tensor_tensor(dst, kept[et][:], fade_rows[:], MULT)
@@ -184,55 +182,58 @@ def tile_attend_lookahead_delivered_lean_kernel(
             width = M // pieces
             for n in range(pieces):
                 cols = slice(width * n, width * (n + 1))
-                nc.vector.tensor_tensor(faded[:, cols], faded[:, cols], delivered[et][:, cols], ADD)
+                vector.tensor_tensor(faded[:, cols], faded[:, cols], delivered[et][:, cols], ADD)
                 nc.sync.dma_start(out=out[P * et : P * (et + 1), cols], in_=faded[:, cols])
 
-        lay_query(0, "vector")
-        lay_query(1, "scalar")
-        quantize(query_codes[0][:], query_scales[0][:], query_bf[0])
-        lay_query(2, "vector")
-        lay_query(3, "scalar")
-        quantize(query_codes[1][:], query_scales[1][:], query_bf[1])
-        score(0, ("vector", "scalar"))
-        look_up_all(0, 0, I, "vector", "vector")
-        quantize(query_codes[2][:], query_scales[2][:], query_bf[2])
-        quantize(query_codes[3][:], query_scales[3][:], query_bf[3])
-        score(1, ("scalar", "scalar"))
+        lay_query(0, vector)
+        lay_query(1, scalar)
+        quantize_query(0)
+        lay_query(2, vector)
+        lay_query(3, scalar)
+        quantize_query(1)
+        score(0, (vector, scalar))
+        look_up(0, 0, I, vector)
+        quantize_query(2)
+        quantize_query(3)
+        score(1, (scalar, scalar))
         combine(0, 0, I, larger[0][:])
-        look_up_all(1, 0, I, "vector", "vector")
-        score(2, ("vector", "scalar"))
-        score(3, ("scalar", "scalar"))
-        nc.gpsimd.tensor_scalar(
+        look_up(1, 0, I, vector)
+        score(2, (vector, scalar))
+        score(3, (scalar, scalar))
+        gpsimd.tensor_scalar(
             laid[:].rearrange("p (e r) -> p e r", r=PACK), msgs_raw[:].rearrange("p r e -> p e r"), 1.0, 0.0, MULT, ADD
         )
         quantize(msgs_codes[:], msgs_scales[:], laid[:])
         combine(1, 0, I, larger[1][:])
-        look_up_all(2, 0, HALF, "scalar")
-        look_up_all(3, 0, HALF, "scalar")
-        fade_old(0, kept[0][:], nc.vector)
+        look_up(2, 0, HALF, scalar)
+        look_up(3, 0, HALF, scalar)
+        fade_old(0, kept[0][:], vector)
         combine(2, 0, HALF, larger[2][:, 0:HALF])
         combine(3, 0, HALF, larger[3][:, 0:HALF])
-        look_up_all(2, HALF, I, "scalar")
-        look_up_all(3, HALF, I, "scalar")
+        look_up(2, HALF, I, scalar)
+        look_up(3, HALF, I, scalar)
         quantize_weights(0)
-        carry(sums[0], [(0, 0, HALF), (1, 0, HALF)], "scalar")
-        deliver(0, 0, HALF, sums[0][:, 0:HALF], "scalar")
-        deliver(1, 0, HALF, sums[0][:, HALF:I], "scalar")
+
+        carry(sums[0][:], [(0, 0, HALF), (1, 0, HALF)], scalar)
+        deliver(0, 0, HALF, sums[0][:, 0:HALF], scalar)
+        deliver(1, 0, HALF, sums[0][:, HALF:I], scalar)
         combine(2, HALF, I, weight[:, 0, 0:HALF])
         combine(3, HALF, I, weight[:, 0, HALF : 2 * HALF])
         quantize_weights(1)
-        fade_old(1, wq_bf[:].bitcast(F32), nc.gpsimd)
-        fade_old(2, kept[1][:], nc.gpsimd)
-        carry(sums[2], [(2, 0, I)], "vector")
-        deliver(2, 0, I, sums[2][:], "vector")
-        carry(sums[1], [(0, HALF, I), (1, HALF, I)], "scalar")
-        deliver(0, HALF, I, sums[1][:, 0:HALF], "scalar")
-        deliver(1, HALF, I, sums[1][:, HALF:I], "scalar")
-        carry(sums[3], [(3, 0, I)], "scalar")
-        deliver(3, 0, HALF, sums[3][:, 0:HALF], "scalar")
-        deliver(3, HALF, I, sums[3][:, HALF:I], "scalar")
-        finish(0, kept[0][:], 1)
-        finish(1, wq_bf[:].bitcast(F32), 1)
-        finish(2, kept[1][:], 1)
-        fade_old(3, kept[2][:], nc.vector)
-        finish(3, kept[2][:], 2)
+        carry(weight[:, 1, 0:HALF], [(2, 0, HALF)], vector)
+        deliver(2, 0, HALF, weight[:, 1, 0:HALF], vector)
+        faded = [kept[0][:], wq_bf[:].bitcast(F32), kept[1][:], kept[2][:]]
+        fade_old(1, faded[1], gpsimd)
+        fade_old(2, faded[2], gpsimd)
+        carry(sums[2][:, 0:HALF], [(2, HALF, I)], vector)
+        deliver(2, HALF, I, sums[2][:, 0:HALF], vector)
+        carry(sums[1][:], [(0, HALF, I), (1, HALF, I)], scalar)
+        deliver(0, HALF, I, sums[1][:, 0:HALF], scalar)
+        deliver(1, HALF, I, sums[1][:, HALF:I], scalar)
+        carry(sums[3][:], [(3, 0, I)], vector)
+        deliver(3, 0, HALF, sums[3][:, 0:HALF], scalar)
+        deliver(3, HALF, I, sums[3][:, HALF:I], scalar)
+        for et in range(E_TILES - 1):
+            finish(et, faded[et], 1)
+        fade_old(3, faded[3], vector)
+        finish(3, faded[3], LAST_PIECES)

from contextlib import ExitStack

import concourse.mybir as mybir

D, T, I, Q, E, M = 512, 1024, 512, 512, 512, 1024
FLOPS = 2 * D * Q * T + 2 * Q * E * I

F32 = mybir.dt.float32
BF16 = mybir.dt.bfloat16
I32 = mybir.dt.int32
U32 = mybir.dt.uint32
U16 = mybir.dt.uint16
U8 = mybir.dt.uint8
FP8X4 = mybir.dt.float8_e4m3fn_x4
FP4X4 = mybir.dt.float4_e2m1fn_x4
MULT = mybir.AluOpType.mult
ADD = mybir.AluOpType.add
MAX = mybir.AluOpType.max
COPY = mybir.ActivationFunctionType.Copy

P = 128
PACK = 4
BANK = 512
BANKS = 8
E_TILES = E // P
QUADS = 4
PER_COL = 16
LINE = 4
HALF = I // 2
LAST_PIECES = 2


def tile_attend_lookahead_delivered_lean_kernel(
    tc, query, keys_words, keys_scales, lam, qs, msgs, old, fade, offs, offs2, offs3, offs4, out
):
    nc = tc.nc
    vector, scalar, gpsimd = nc.vector, nc.scalar, nc.gpsimd
    with ExitStack() as ctx:
        keep = ctx.enter_context(tc.tile_pool(name="keep", bufs=1))
        psum = ctx.enter_context(tc.psum_pool(name="psum", bufs=BANKS))

        def tiles(name, count, shape, dtype):
            return [keep.tile(shape, dtype, name="%s%d" % (name, n), align_bytes=64) for n in range(count)]

        key_scales = keep.tile([P, T], U8, align_bytes=64)
        for quad in range(QUADS):
            nc.scalar.dma_start(
                out=key_scales[32 * quad : 32 * quad + 4, :].bitcast(I32),
                in_=keys_scales[0, 4 * quad : 4 * quad + 4, :].bitcast(I32),
            )
        query_raw = keep.tile([P, PACK, Q], F32)
        nc.sync.dma_start(out=query_raw[:], in_=query.rearrange("(p j) q -> p j q", j=PACK))
        key_words = keep.tile([P, 2 * T], U8, align_bytes=64)
        nc.sync.dma_start(out=key_words[:].bitcast(I32), in_=keys_words[0].bitcast(I32))
        second = keep.tile([P, I // PER_COL], U16)
        nc.sync.dma_start(second[:], offs2)
        first = keep.tile([P, I // PER_COL], U16)
        nc.sync.dma_start(first[:], offs)
        msgs_raw = keep.tile([P, PACK, E], F32)
        nc.sync.dma_start(out=msgs_raw[:], in_=msgs.rearrange("(p r) e -> p r e", r=PACK))
        third = keep.tile([P, I // PER_COL], U16)
        nc.sync.dma_start(third[:], offs3)
        kept = tiles("kept", E_TILES, [P, M], F32)
        nc.sync.dma_start(out=kept[0][:], in_=old[0:P, :])
        lam_sb = keep.tile([P, PACK], F32)
        nc.sync.dma_start(out=lam_sb[:], in_=lam.rearrange("(p r) o -> p (r o)", r=PACK))
        qs_sb = keep.tile([P, PACK], F32)
        nc.sync.dma_start(out=qs_sb[:], in_=qs.rearrange("(p r) o -> p (r o)", r=PACK))
        fade_rows = keep.tile([P, M], F32)
        nc.sync.dma_start(out=fade_rows[:], in_=fade[0].partition_broadcast(P))
        for et in range(1, E_TILES):
            nc.sync.dma_start(out=kept[et][:], in_=old[P * et : P * (et + 1), :])
        places = keep.tile([P, I // PER_COL], U16)
        nc.sync.dma_start(places[:], offs4)

        delivered = tiles("delivered", E_TILES, [P, M], F32)
        for et in range(E_TILES):
            (vector if et < E_TILES // 2 else gpsimd).memset(delivered[et][:], 0.0)

        laid = keep.tile([P, E * PACK], BF16, align_bytes=64)
        query_bf = [laid[:, P * PACK * place : P * PACK * (place + 1)] for place in (0, 1, 0, 2)]
        query_codes = tiles("query_codes", PACK, [P, P], U32)
        query_scales = tiles("query_scales", PACK, [P, P], U8)
        scores = tiles("scores", PACK, [P, T], F32)
        own = tiles("own", PACK, [P, I], F32)
        next_a = tiles("next_a", PACK, [P, I], F32)
        next_b = tiles("next_b", PACK, [P, I], F32)
        larger = tiles("larger", PACK, [P, I], F32)
        weight = keep.tile([P, 2, PACK * HALF], F32)
        wq_bf = keep.tile([P, I * PACK], BF16, align_bytes=64)
        wq_codes = keep.tile([P, I], U32, align_bytes=64)
        wq_scales = keep.tile([P, I], U8, align_bytes=64)
        msgs_codes = keep.tile([P, E], U32, align_bytes=64)
        msgs_scales = keep.tile([P, E], U8, align_bytes=64)
        sums = tiles("sums", E_TILES, [P, I], F32)

        def copy(engine, dst, src):
            if engine is vector:
                vector.tensor_copy(out=dst, in_=src)
            else:
                scalar.copy(out=dst, in_=src)

        def copy_listed(engine, dst, src):
            if engine is vector:
                vector.tensor_copy(dst, src)
            else:
                scalar.activation(dst, src, COPY)

        def quantize(codes, scales, values):
            vector.quantize_mx(out=codes.bitcast(FP8X4), scales=scales, in_=values)

        def lay_query(r, engine):
            src = query_raw[:].rearrange("p j (s r) -> p r s j", r=PACK)[:, r]
            copy(engine, query_bf[r].rearrange("p (s j) -> p s j", j=PACK), src)

        def quantize_query(r):
            quantize(query_codes[r][:], query_scales[r][:], query_bf[r])

        def score(r, engines):
            for n, engine in enumerate(engines):
                bank = psum.tile([P, BANK], F32, name="bank")
                nc.tensor.matmul_mx(
                    out=bank[:],
                    lhsT=query_codes[r][:].bitcast(FP8X4),
                    lhsT_scale=query_scales[r][:],
                    rhs=key_words[:, 2 * BANK * n : 2 * BANK * (n + 1)].bitcast(FP4X4),
                    rhs_scale=key_scales[:, BANK * n : BANK * (n + 1)],
                    start=True,
                    stop=True,
                )
                copy(engine, scores[r][:, BANK * n : BANK * (n + 1)], bank[:])

        def look_up(r, lo, hi, engine):
            for dst, offsets, by in ((next_a, second, scalar), (next_b, third, engine), (own, first, engine)):
                copy_listed(by, dst[r][:, lo:hi], scores[r][:].indirect(offsets[:, lo // PER_COL : hi // PER_COL]))

        def combine(r, lo, hi, scratch):
            vector.tensor_tensor(scratch, next_a[r][:, lo:hi], next_b[r][:, lo:hi], MAX)
            vector.scalar_tensor_tensor(
                weight[:, lo // HALF : hi // HALF, HALF * r : HALF * (r + 1)],
                scratch.rearrange("p (h i) -> p h i", i=HALF),
                lam_sb[:, r : r + 1],
                own[r][:, lo:hi].rearrange("p (h i) -> p h i", i=HALF),
                MULT,
                ADD,
            )

        def quantize_weights(h):
            values = wq_bf[:, HALF * PACK * h : HALF * PACK * (h + 1)]
            vector.tensor_tensor(
                values.rearrange("p (c i r) -> p c r i", i=LINE, r=PACK),
                weight[:, h, :].rearrange("p (r c i) -> p c r i", r=PACK, i=LINE),
                qs_sb[:].unsqueeze(1).unsqueeze(3).to_broadcast([P, HALF // LINE, PACK, LINE]),
                MULT,
            )
            quantize(wq_codes[:, HALF * h : HALF * (h + 1)], wq_scales[:, HALF * h : HALF * (h + 1)], values)

        def carry(dst, parts, engine):
            bank = psum.tile([P, BANK], F32, name="bank")
            filled = 0
            for et, lo, hi in parts:
                cols = slice(P * et, P * (et + 1))
                nc.tensor.matmul_mx(
                    out=bank[:, filled : filled + hi - lo],
                    lhsT=msgs_codes[:, cols].bitcast(FP8X4),
                    lhsT_scale=msgs_scales[:, cols],
                    rhs=wq_codes[:, lo:hi].bitcast(FP8X4),
                    rhs_scale=wq_scales[:, lo:hi],
                    start=True,
                    stop=True,
                )
                filled = filled + hi - lo
            copy(engine, dst, bank[:, 0:filled])

        def deliver(et, lo, hi, src, engine):
            copy_listed(engine, delivered[et][:].indirect(places[:, lo // PER_COL : hi // PER_COL]), src)

        def fade_old(et, dst, engine):
            engine.tensor_tensor(dst, kept[et][:], fade_rows[:], MULT)

        def finish(et, faded, pieces):
            width = M // pieces
            for n in range(pieces):
                cols = slice(width * n, width * (n + 1))
                vector.tensor_tensor(faded[:, cols], faded[:, cols], delivered[et][:, cols], ADD)
                nc.sync.dma_start(out=out[P * et : P * (et + 1), cols], in_=faded[:, cols])

        lay_query(0, vector)
        lay_query(1, scalar)
        quantize_query(0)
        lay_query(2, vector)
        lay_query(3, scalar)
        quantize_query(1)
        score(0, (vector, scalar))
        look_up(0, 0, I, vector)
        quantize_query(2)
        quantize_query(3)
        score(1, (scalar, scalar))
        combine(0, 0, I, larger[0][:])
        look_up(1, 0, I, vector)
        score(2, (vector, scalar))
        score(3, (scalar, scalar))
        gpsimd.tensor_scalar(
            laid[:].rearrange("p (e r) -> p e r", r=PACK), msgs_raw[:].rearrange("p r e -> p e r"), 1.0, 0.0, MULT, ADD
        )
        quantize(msgs_codes[:], msgs_scales[:], laid[:])
        combine(1, 0, I, larger[1][:])
        look_up(2, 0, HALF, scalar)
        look_up(3, 0, HALF, scalar)
        fade_old(0, kept[0][:], vector)
        combine(2, 0, HALF, larger[2][:, 0:HALF])
        combine(3, 0, HALF, larger[3][:, 0:HALF])
        look_up(2, HALF, I, scalar)
        look_up(3, HALF, I, scalar)
        quantize_weights(0)

        carry(sums[0][:], [(0, 0, HALF), (1, 0, HALF)], scalar)
        deliver(0, 0, HALF, sums[0][:, 0:HALF], scalar)
        deliver(1, 0, HALF, sums[0][:, HALF:I], scalar)
        combine(2, HALF, I, weight[:, 0, 0:HALF])
        combine(3, HALF, I, weight[:, 0, HALF : 2 * HALF])
        quantize_weights(1)
        carry(weight[:, 1, 0:HALF], [(2, 0, HALF)], vector)
        deliver(2, 0, HALF, weight[:, 1, 0:HALF], vector)
        faded = [kept[0][:], wq_bf[:].bitcast(F32), kept[1][:], kept[2][:]]
        fade_old(1, faded[1], gpsimd)
        fade_old(2, faded[2], gpsimd)
        carry(sums[2][:, 0:HALF], [(2, HALF, I)], vector)
        deliver(2, HALF, I, sums[2][:, 0:HALF], vector)
        carry(sums[1][:], [(0, HALF, I), (1, HALF, I)], scalar)
        deliver(0, HALF, I, sums[1][:, 0:HALF], scalar)
        deliver(1, HALF, I, sums[1][:, HALF:I], scalar)
        carry(sums[3][:], [(3, 0, I)], vector)
        deliver(3, 0, HALF, sums[3][:, 0:HALF], scalar)
        deliver(3, HALF, I, sums[3][:, HALF:I], scalar)
        for et in range(E_TILES - 1):
            finish(et, faded[et], 1)
        fade_old(3, faded[3], vector)
        finish(3, faded[3], LAST_PIECES)
